import numpy as np
import ml_dtypes


def mxq(x, axis, fmt="e4m3"):
    dtype, down = {"e4m3": (ml_dtypes.float8_e4m3fn, 7), "e5m2": (ml_dtypes.float8_e5m2, 14)}[fmt]
    v = np.moveaxis(np.asarray(x, np.float32).astype(ml_dtypes.bfloat16).astype(np.float64), axis, -1)
    blocks = v.reshape(v.shape[:-1] + (-1, 32))
    amax = np.abs(blocks).max(-1, keepdims=True)
    byte = np.maximum(np.where(amax > 0, np.frexp(amax)[1] - 1 + 127, 0) - down, 1)
    scale = np.exp2(byte - 127.0)
    codes = (blocks / scale).astype(np.float32).astype(dtype).astype(np.float64)
    return np.moveaxis((codes * scale).reshape(v.shape), -1, axis)


WIDE = False


def mx_kscale(k):
    if not WIDE:
        return np.ones(k)
    levels = np.array([10, -10, 5, -5, 0])
    if k % 512:
        return np.exp2(np.random.permutation(np.resize(levels, k // 32))).repeat(32)
    a = np.empty((k // 512, 16))
    for p in range(k // 512):
        a[p, :8] = np.random.permutation(np.resize(levels, 8))
        for g in range(8):
            far = levels[np.abs(levels - a[p, g]) >= 10]
            a[p, g + 8] = far[np.random.randint(len(far))]
    return np.exp2(a.ravel()).repeat(32)


def f64(x):
    return np.asarray(x).astype(np.float64)


def striped(idx):
    return np.tile(idx.reshape(-1, 16).T, (8, 1)).astype(np.uint16)


def unstriped(offs):
    return offs[:16].T.reshape(-1).astype(np.int64)


def striped8(idx):
    return np.concatenate([x.reshape(-1, 16).T for x in idx]).astype(np.uint16)


def runs(offs, k):
    lists = np.stack([offs[16 * r : 16 * r + 16].T.reshape(-1) for r in range(8)]).astype(np.int64)
    return lists[np.arange(k) % 512 // 64]


def pack_weight(w):
    k, n = w.shape
    w = f64(np.asarray(w, np.float32).astype(ml_dtypes.bfloat16)).reshape(k // 32, 32, n)
    amax = np.abs(w).max(1)
    byte = np.clip(np.where(amax > 0, np.frexp(amax)[1] - 1 + 127 - 7, 1), 1, 254)
    scaled = (w * np.exp2(127.0 - byte)[:, None, :]).reshape(k, n).astype(np.float32)
    words = np.ascontiguousarray(scaled.reshape(k // 512, 128, 4, n).transpose(0, 1, 3, 2)).astype(ml_dtypes.float8_e4m3fn).view(np.uint8)
    return words, np.ascontiguousarray(byte.astype(np.uint8).reshape(k // 512, 16, n))


def unpack_weight(words, scales):
    g, p, n, _ = words.shape
    vals = np.ascontiguousarray(words).view(ml_dtypes.float8_e4m3fn).astype(np.float64) * np.repeat(np.exp2(scales.astype(np.float64) - 127.0), 8, axis=1)[..., None]
    return vals.transpose(0, 1, 3, 2).reshape(g * 512, n)


E2M1 = np.array([0.0, 0.5, 1.0, 1.5, 2.0, 3.0, 4.0, 6.0, -0.0, -0.5, -1.0, -1.5, -2.0, -3.0, -4.0, -6.0])


def pack_fp4(w):
    k, n = w.shape
    w = f64(np.asarray(w, np.float32).astype(ml_dtypes.bfloat16)).reshape(k // 32, 32, n)
    amax = np.abs(w).max(1)
    mant, ex = np.frexp(amax / 6.0)
    byte = np.clip(np.where(amax > 0, np.where(mant > 0.5, ex, ex - 1) + 127, 1), 1, 254)
    scaled = (w * np.exp2(127.0 - byte)[:, None, :]).reshape(k, n).astype(np.float32)
    c = np.ascontiguousarray(scaled.reshape(k // 512, 128, 4, n).transpose(0, 1, 3, 2)).astype(ml_dtypes.float4_e2m1fn).view(np.uint8) & 0xF
    words = (c[..., 0::2] | (c[..., 1::2] << 4)).reshape(k // 512, 128, 2 * n)
    return np.ascontiguousarray(words), np.ascontiguousarray(byte.astype(np.uint8).reshape(k // 512, 16, n))


def unpack_fp4(words, scales):
    g, _, n = scales.shape
    words = np.ascontiguousarray(words).reshape(g, 128, n, 2)
    nib = np.empty((g, 128, n, 4), np.uint8)
    nib[..., 0::2] = words & 0xF
    nib[..., 1::2] = words >> 4
    vals = E2M1[nib] * np.repeat(np.exp2(scales.astype(np.float64) - 127.0), 8, axis=1)[..., None]
    return vals.transpose(0, 1, 3, 2).reshape(g * 512, n)


def sigmoid(v):
    return 1.0 / (1.0 + np.exp(-np.maximum(v, -700.0)))


K, T, S, N, G, H, U = 512, 2048, 256, 512, 2048, 512, 512


def setup_inputs():
    n = np.random.standard_normal
    s = mx_kscale(K)[:, None]
    u = mx_kscale(K)
    packed_xT = pack_weight(n((K, T)) * s)
    packed_dT = pack_weight(n((K, G)) / s)
    packed_w1 = pack_fp4(n((H, N)) / np.sqrt(H) / u[:, None])
    perm = np.random.permutation(U)
    return {
        "x_words": packed_xT[0],
        "x_scales": packed_xT[1],
        "d_words": packed_dT[0],
        "d_scales": packed_dT[1],
        "sl": np.random.uniform(1.0, 2.0, (H, 1)).astype(np.float32),
        "th": (0.5 * n((H, 1))).astype(np.float32),
        "gn": (np.random.uniform(0.5, 1.5, (H, 1)) * u[:, None]).astype(np.float32),
        "w1_words": packed_w1[0],
        "w1_scales": packed_w1[1],
        "offs": striped8(np.random.randint(0, T, (8, S))),
        "k1": striped8(np.random.randint(0, G, (8, H))),
        "n1": striped8(np.stack([np.random.permutation(S) for _ in range(8)])),
        "n2": striped(perm[:S]),
        "n3": striped(perm[S:]),
        "n4": striped(np.random.permutation(U)),
    }


def reference(x_words, x_scales, d_words, d_scales, sl, th, gn, w1_words, w1_scales, offs, k1, n1, n2, n3, n4):
    d_k1 = unpack_weight(d_words, d_scales)[np.arange(K)[:, None], runs(k1, K)]
    xq = unpack_weight(x_words, x_scales)[np.arange(K)[:, None], runs(offs, K)]
    h = 0.0625 * (d_k1.T @ xq)
    sg = sigmoid(f64(sl) * (h[np.arange(H)[:, None], runs(n1, H)] - f64(th)))
    z = f64(gn) * (h * sg)
    h2 = unpack_fp4(w1_words, w1_scales).T @ mxq(z, 0, "e4m3")
    nw = 0.5 * h2
    ph = np.zeros((N, U))
    ph[:, unstriped(n2)] = h2
    pg = ph.copy()
    pg[:, unstriped(n3)] = nw
    return pg - pg[:, unstriped(n4)]

@@ -1,0 +1,194 @@
+from contextlib import ExitStack
+
+import concourse.mybir as mybir
+
+F32 = mybir.dt.float32
+BF16 = mybir.dt.bfloat16
+I32 = mybir.dt.int32
+U32 = mybir.dt.uint32
+U16 = mybir.dt.uint16
+U8 = mybir.dt.uint8
+FP8X4 = mybir.dt.float8_e4m3fn_x4
+FP4X4 = mybir.dt.float4_e2m1fn_x4
+ACT = mybir.ActivationFunctionType
+ALU = mybir.AluOpType
+
+P = 128
+PACK = 4
+TABLE = 2048
+S = 256
+H = 512
+N = 512
+U = 512
+HALF = 128
+TILES = 4
+
+FLOPS = 2 * 512 * H * S + 2 * H * N * S
+
+
+def tile_picked_hpqesapagtwo_none_p_kernel(
+    tc, x_words, x_scales, d_words, d_scales, sl, th, gn, w1_words, w1_scales, offs, k1, n1, n2, n3, n4, out
+):
+    nc = tc.nc
+    with ExitStack() as ctx:
+        keep = ctx.enter_context(tc.tile_pool(name="keep", bufs=1))
+        psum = ctx.enter_context(tc.psum_pool(name="psum", bufs=1))
+
+        k1_t = keep.tile([P, H // 16], U16, name="k1_t")
+        offs_t = keep.tile([P, S // 16], U16, name="offs_t")
+        n1_t = keep.tile([P, S // 16], U16, name="n1_t")
+        n2_t = keep.tile([P, S // 16], U16, name="n2_t")
+        n3_t = keep.tile([P, S // 16], U16, name="n3_t")
+        n4_t = keep.tile([P, U // 16], U16, name="n4_t")
+        d_table = keep.tile([P, TABLE], U32, name="d_table", align_bytes=64)
+        x_table = keep.tile([P, TABLE], U32, name="x_table", align_bytes=64)
+        nc.sync.dma_start(k1_t[:], k1)
+        nc.sync.dma_start(offs_t[:], offs)
+        nc.sync.dma_start(d_table[:].bitcast(I32), d_words[0].rearrange("p n t -> p (n t)").bitcast(I32))
+        nc.sync.dma_start(n1_t[:], n1)
+        nc.sync.dma_start(n2_t[:], n2)
+        nc.sync.dma_start(n3_t[:], n3)
+        nc.sync.dma_start(x_table[:].bitcast(I32), x_words[0].rearrange("p n t -> p (n t)").bitcast(I32))
+        nc.sync.dma_start(n4_t[:], n4)
+
+        d_stable = keep.tile([P, TABLE], U8, name="d_stable", align_bytes=64)
+        x_stable = keep.tile([P, TABLE], U8, name="x_stable", align_bytes=64)
+        planes = keep.tile([P, H + S + N], U8, name="planes", align_bytes=64)
+        d_plane = planes[:, 0:H]
+        x_plane = planes[:, H : H + S]
+        nc.vector.memset(d_stable[:].bitcast(I32), 0)
+        nc.scalar.dma_start(d_stable[0:P:8, :].bitcast(I32), d_scales[0].bitcast(I32))
+        nc.vector.memset(x_stable[:].bitcast(I32), 0)
+        nc.scalar.dma_start(x_stable[0:P:8, :].bitcast(I32), x_scales[0].bitcast(I32))
+        nc.gpsimd.dma_start(planes[0:P:8, H + S :].bitcast(I32), w1_scales[0].bitcast(I32))
+
+        sl_t = keep.tile([P, PACK], F32, name="sl_t")
+        th_t = keep.tile([P, PACK], F32, name="th_t")
+        gn_t = keep.tile([P, PACK], F32, name="gn_t")
+        bias_t = keep.tile([P, PACK], F32, name="bias_t")
+        w_codes = keep.tile([P, 2 * N], U8, name="w_codes", align_bytes=64)
+        nc.gpsimd.dma_start(sl_t[:], sl.rearrange("(p t) o -> p (t o)", t=PACK))
+        nc.gpsimd.dma_start(th_t[:], th.rearrange("(p t) o -> p (t o)", t=PACK))
+        nc.gpsimd.dma_start(gn_t[:], gn.rearrange("(p t) o -> p (t o)", t=PACK))
+        nc.gpsimd.dma_start(w_codes[:].bitcast(I32), w1_words[0].bitcast(I32))
+
+        d_sgot = keep.tile([P, H], U8, name="d_sgot", align_bytes=64)
+        x_sgot = keep.tile([P, S], U8, name="x_sgot", align_bytes=64)
+        nc.vector.tensor_copy(d_sgot[:], d_stable[:].indirect(k1_t[:]))
+        nc.vector.tensor_copy(x_sgot[:], x_stable[:].indirect(offs_t[:]))
+        nc.vector.tensor_copy(
+            d_plane.rearrange("p (t m) -> p t m", t=PACK), d_sgot[:].rearrange("p (m t) -> p t m", t=PACK)
+        )
+        nc.vector.tensor_copy(x_plane.bitcast(I32), x_sgot[:].bitcast(I32))
+        for b in range(1, 4):
+            nc.scalar.dma_start(planes[b:P:32, :].bitcast(I32), planes[8 * b : P : 32, :].bitcast(I32))
+
+        d_got = keep.tile([P, H], U32, name="d_got", align_bytes=64)
+        d_codes = keep.tile([P, H], U32, name="d_codes", align_bytes=64)
+        x_codes = keep.tile([P, S], U32, name="x_codes", align_bytes=64)
+        nc.vector.tensor_copy(d_got[:], d_table[:].indirect(k1_t[:]))
+        nc.vector.scalar_tensor_tensor(bias_t[:], sl_t[:], -1.0, th_t[:], ALU.mult, ALU.mult)
+        nc.vector.tensor_copy(
+            d_codes[:].rearrange("p (t c i) -> p c t i", t=PACK, i=4),
+            d_got[:].rearrange("p (c i t) -> p c t i", t=PACK, i=4),
+        )
+        nc.vector.tensor_copy(x_codes[:], x_table[:].indirect(offs_t[:]))
+
+        h = []
+        for t in range(PACK):
+            acc = psum.tile([P, S], F32, name="h_acc%d" % t)
+            nc.tensor.matmul_mx(
+                out=acc[:],
+                lhsT=d_codes[:, t * P : (t + 1) * P].bitcast(FP8X4),
+                lhsT_scale=planes[:, t * P : (t + 1) * P],
+                rhs=x_codes[:].bitcast(FP8X4),
+                rhs_scale=x_plane,
+                start=True,
+                stop=True,
+            )
+            h_t = keep.tile([P, S], F32, name="h%d" % t)
+            nc.vector.tensor_scalar(h_t[:], acc[:], 0.0625, None, ALU.mult)
+            h.append(h_t)
+
+        h2_acc = [psum.tile([P, S], F32, name="h2_acc%d" % m) for m in range(TILES)]
+        h2 = [keep.tile([P, S], F32, name="h2_%d" % m) for m in range(TILES)]
+
+        def gate(u):
+            cols = slice(u * HALF, (u + 1) * HALF)
+            sg = keep.tile([P, PACK, HALF], F32, name="sg%d" % u)
+            z_rows = keep.tile([P, PACK, HALF], BF16, name="z_rows%d" % u, align_bytes=64)
+            z_woven = keep.tile([P, HALF, PACK], BF16, name="z_woven%d" % u, align_bytes=64)
+            z_codes = keep.tile([P, HALF], U32, name="z_codes%d" % u, align_bytes=64)
+            z_plane = keep.tile([P, HALF], U8, name="z_plane%d" % u, align_bytes=64)
+            for t in range(PACK):
+                nc.scalar.activation(
+                    out=sg[:, t, :],
+                    in_=h[t][:].indirect(n1_t[:, u * HALF // 16 : (u + 1) * HALF // 16]),
+                    func=ACT.Sigmoid,
+                    scale=sl_t[:, t : t + 1],
+                    bias=bias_t[:, t : t + 1],
+                )
+                nc.vector.scalar_tensor_tensor(
+                    z_rows[:, t, :], h[t][:, cols], gn_t[:, t : t + 1], sg[:, t, :], ALU.mult, ALU.mult
+                )
+            nc.vector.tensor_copy(
+                z_woven[:].rearrange("p (c i) t -> p c t i", i=4), z_rows[:].rearrange("p t (c i) -> p c t i", i=4)
+            )
+            nc.vector.quantize_mx(
+                out=z_codes[:].bitcast(FP8X4), scales=z_plane[:], in_=z_woven[:].rearrange("p j t -> p (j t)")
+            )
+            return z_codes, z_plane
+
+        def second_product(u, z_codes, z_plane):
+            cols = slice(u * HALF, (u + 1) * HALF)
+            for m in range(TILES):
+                nc.tensor.matmul_mx(
+                    out=h2_acc[m][:, cols],
+                    lhsT=w_codes[:, 2 * m * P : 2 * (m + 1) * P].bitcast(FP4X4),
+                    lhsT_scale=planes[:, H + S + m * P : H + S + (m + 1) * P],
+                    rhs=z_codes[:].bitcast(FP8X4),
+                    rhs_scale=z_plane[:],
+                    start=True,
+                    stop=True,
+                )
+
+        second_product(0, *gate(0))
+        z_last = gate(1)
+        for m in (0, 1):
+            nc.scalar.copy(h2[m][:, 0:HALF], h2_acc[m][:, 0:HALF])
+        second_product(1, *z_last)
+        for m in (0, 1):
+            nc.vector.tensor_copy(h2[m][:, HALF:], h2_acc[m][:, HALF:])
+        for m in (2, 3):
+            nc.vector.tensor_copy(h2[m][:], h2_acc[m][:])
+
+        pg = [keep.tile([P, U], F32, name="pg%d" % m) for m in range(TILES)]
+
+        def scatter(m, places, factor, lo, hi):
+            nc.scalar.activation(
+                out=pg[m][:].indirect(places[:, lo // 16 : hi // 16]), in_=h2[m][:, lo:hi], func=ACT.Copy, scale=factor
+            )
+
+        def finish(m, bounds):
+            got = keep.tile([P, U], F32, name="got%d" % m)
+            res = keep.tile([P, U], F32, name="res%d" % m)
+            for lo, hi in bounds:
+                nc.scalar.activation(
+                    out=got[:, lo:hi], in_=pg[m][:].indirect(n4_t[:, lo // 16 : hi // 16]), func=ACT.Copy
+                )
+                nc.vector.tensor_tensor(res[:, lo:hi], pg[m][:, lo:hi], got[:, lo:hi], ALU.subtract)
+                nc.sync.dma_start(out[m * P : (m + 1) * P, lo:hi], res[:, lo:hi])
+
+        halves = [(0, 256), (256, 512)]
+        for lo in (0, HALF):
+            for places, factor in ((n2_t, 1.0), (n3_t, 0.5)):
+                for m in (0, 1):
+                    scatter(m, places, factor, lo, lo + HALF)
+        finish(0, halves)
+        scatter(2, n2_t, 1.0, 0, S)
+        finish(1, halves)
+        scatter(3, n2_t, 1.0, 0, S)
+        scatter(2, n3_t, 0.5, 0, S)
+        scatter(3, n3_t, 0.5, 0, S)
+        finish(2, halves)
+        finish(3, [(0, 256), (256, 384), (384, 512)])

@@ -41,58 +41,63 @@ def tile_picked_hpqesapagtwo_none_p_kernel(
         n3_t = keep.tile([P, S // 16], U16, name="n3_t")
         n4_t = keep.tile([P, U // 16], U16, name="n4_t")
         d_table = keep.tile([P, TABLE], U32, name="d_table", align_bytes=64)
-        x_table = keep.tile([P, TABLE], U32, name="x_table", align_bytes=64)
-        nc.sync.dma_start(k1_t[:], k1)
-        nc.sync.dma_start(offs_t[:], offs)
-        nc.sync.dma_start(d_table[:].bitcast(I32), d_words[0].rearrange("p n t -> p (n t)").bitcast(I32))
-        nc.sync.dma_start(n1_t[:], n1)
-        nc.sync.dma_start(n2_t[:], n2)
-        nc.sync.dma_start(n3_t[:], n3)
-        nc.sync.dma_start(x_table[:].bitcast(I32), x_words[0].rearrange("p n t -> p (n t)").bitcast(I32))
-        nc.sync.dma_start(n4_t[:], n4)
-
+        x_table = keep.tile([P, TABLE], U32, name="x_table", tag="x_table", align_bytes=64)
         d_stable = keep.tile([P, TABLE], U8, name="d_stable", align_bytes=64)
+        nc.sync.dma_start(k1_t[:], k1)
+        nc.sync.dma_start(
+            d_stable[:].bitcast(I32), d_scales[0].bitcast(I32).unsqueeze(1).to_broadcast([16, 8, TABLE // 4])
+        )
         x_stable = keep.tile([P, TABLE], U8, name="x_stable", align_bytes=64)
-        planes = keep.tile([P, H + S + N], U8, name="planes", align_bytes=64)
-        d_plane = planes[:, 0:H]
-        x_plane = planes[:, H : H + S]
-        nc.vector.memset(d_stable[:].bitcast(I32), 0)
-        nc.scalar.dma_start(d_stable[0:P:8, :].bitcast(I32), d_scales[0].bitcast(I32))
-        nc.vector.memset(x_stable[:].bitcast(I32), 0)
-        nc.scalar.dma_start(x_stable[0:P:8, :].bitcast(I32), x_scales[0].bitcast(I32))
-        nc.gpsimd.dma_start(planes[0:P:8, H + S :].bitcast(I32), w1_scales[0].bitcast(I32))
-
+        nc.sync.dma_start(offs_t[:], offs)
+        nc.sync.dma_start(
+            x_stable[:].bitcast(I32), x_scales[0].bitcast(I32).unsqueeze(1).to_broadcast([16, 8, TABLE // 4])
+        )
+        spread = keep.tile([P, H + S + N], U8, name="spread", align_bytes=64)
+        nc.sync.dma_start(spread[0:P:8, H + S :].bitcast(I32), w1_scales[0].bitcast(I32))
         sl_t = keep.tile([P, PACK], F32, name="sl_t")
         th_t = keep.tile([P, PACK], F32, name="th_t")
-        gn_t = keep.tile([P, PACK], F32, name="gn_t")
-        bias_t = keep.tile([P, PACK], F32, name="bias_t")
-        w_codes = keep.tile([P, 2 * N], U8, name="w_codes", align_bytes=64)
         nc.gpsimd.dma_start(sl_t[:], sl.rearrange("(p t) o -> p (t o)", t=PACK))
         nc.gpsimd.dma_start(th_t[:], th.rearrange("(p t) o -> p (t o)", t=PACK))
+        nc.sync.dma_start(d_table[:].bitcast(I32), d_words[0].rearrange("p n t -> p (n t)").bitcast(I32))
+        nc.sync.dma_start(n1_t[:], n1)
+        nc.sync.dma_start(x_table[:].bitcast(I32), x_words[0].rearrange("p n t -> p (n t)").bitcast(I32))
+        nc.sync.dma_start(n2_t[:], n2)
+        nc.sync.dma_start(n3_t[:], n3)
+        nc.sync.dma_start(n4_t[:], n4)
+
+        planes = keep.tile([P, H + S + N], U8, name="planes", align_bytes=64)
+        x_plane = planes[:, H : H + S]
+
+        gn_t = keep.tile([P, PACK], F32, name="gn_t")
+        w_codes = keep.tile([P, 2 * N], U8, name="w_codes", align_bytes=64)
         nc.gpsimd.dma_start(gn_t[:], gn.rearrange("(p t) o -> p (t o)", t=PACK))
         nc.gpsimd.dma_start(w_codes[:].bitcast(I32), w1_words[0].bitcast(I32))
 
         d_sgot = keep.tile([P, H], U8, name="d_sgot", align_bytes=64)
-        x_sgot = keep.tile([P, S], U8, name="x_sgot", align_bytes=64)
+        x_sgot = keep.tile([P, S], U8, name="x_sgot", tag="got", align_bytes=64)
         nc.vector.tensor_copy(d_sgot[:], d_stable[:].indirect(k1_t[:]))
-        nc.vector.tensor_copy(x_sgot[:], x_stable[:].indirect(offs_t[:]))
         nc.vector.tensor_copy(
-            d_plane.rearrange("p (t m) -> p t m", t=PACK), d_sgot[:].rearrange("p (m t) -> p t m", t=PACK)
+            spread[:, 0:H].rearrange("p (t m) -> p t m", t=PACK), d_sgot[:].rearrange("p (m t) -> p t m", t=PACK)
         )
-        nc.vector.tensor_copy(x_plane.bitcast(I32), x_sgot[:].bitcast(I32))
-        for b in range(1, 4):
-            nc.scalar.dma_start(planes[b:P:32, :].bitcast(I32), planes[8 * b : P : 32, :].bitcast(I32))
+        nc.vector.tensor_copy(x_sgot[:], x_stable[:].indirect(offs_t[:]))
+        nc.vector.tensor_copy(spread[:, H : H + S].bitcast(I32), x_sgot[:].bitcast(I32))
+        for q in range(4):
+            nc.scalar.dma_start(
+                planes[32 * q : 32 * q + 4, :].bitcast(I32), spread[32 * q : 32 * q + 32 : 8, :].bitcast(I32)
+            )
 
-        d_got = keep.tile([P, H], U32, name="d_got", align_bytes=64)
+        d_got = keep.tile([P, H], U32, name="d_got", tag="got", align_bytes=64)
         d_codes = keep.tile([P, H], U32, name="d_codes", align_bytes=64)
-        x_codes = keep.tile([P, S], U32, name="x_codes", align_bytes=64)
+        x_codes = keep.tile([P, S], U32, name="x_codes", tag="got", align_bytes=64)
         nc.vector.tensor_copy(d_got[:], d_table[:].indirect(k1_t[:]))
-        nc.vector.scalar_tensor_tensor(bias_t[:], sl_t[:], -1.0, th_t[:], ALU.mult, ALU.mult)
         nc.vector.tensor_copy(
             d_codes[:].rearrange("p (t c i) -> p c t i", t=PACK, i=4),
             d_got[:].rearrange("p (c i t) -> p c t i", t=PACK, i=4),
         )
         nc.vector.tensor_copy(x_codes[:], x_table[:].indirect(offs_t[:]))
+
+        bias_t = keep.tile([P, PACK], F32, name="bias_t", tag="x_table", align_bytes=64)
+        nc.vector.scalar_tensor_tensor(bias_t[:], sl_t[:], -1.0, th_t[:], ALU.mult, ALU.mult)
 
         h = []
         for t in range(PACK):
@@ -116,8 +121,8 @@ def tile_picked_hpqesapagtwo_none_p_kernel(
         def gate(u):
             cols = slice(u * HALF, (u + 1) * HALF)
             sg = keep.tile([P, PACK, HALF], F32, name="sg%d" % u)
-            z_rows = keep.tile([P, PACK, HALF], BF16, name="z_rows%d" % u, align_bytes=64)
-            z_woven = keep.tile([P, HALF, PACK], BF16, name="z_woven%d" % u, align_bytes=64)
+            z_rows = keep.tile([P, PACK, HALF], BF16, name="z_rows%d" % u, tag="z%d" % u, align_bytes=64)
+            z_woven = keep.tile([P, HALF, PACK], BF16, name="z_woven%d" % u, tag="z%d" % (u + 1), align_bytes=64)
             z_codes = keep.tile([P, HALF], U32, name="z_codes%d" % u, align_bytes=64)
             z_plane = keep.tile([P, HALF], U8, name="z_plane%d" % u, align_bytes=64)
             for t in range(PACK):

from contextlib import ExitStack

import concourse.mybir as mybir

F32 = mybir.dt.float32
BF16 = mybir.dt.bfloat16
I32 = mybir.dt.int32
U32 = mybir.dt.uint32
U16 = mybir.dt.uint16
U8 = mybir.dt.uint8
FP8X4 = mybir.dt.float8_e4m3fn_x4
FP4X4 = mybir.dt.float4_e2m1fn_x4
ACT = mybir.ActivationFunctionType
ALU = mybir.AluOpType

P = 128
PACK = 4
TABLE = 2048
S = 256
H = 512
N = 512
U = 512
HALF = 128
TILES = 4

FLOPS = 2 * 512 * H * S + 2 * H * N * S


def tile_picked_hpqesapagtwo_none_p_kernel(
    tc, x_words, x_scales, d_words, d_scales, sl, th, gn, w1_words, w1_scales, offs, k1, n1, n2, n3, n4, out
):
    nc = tc.nc
    with ExitStack() as ctx:
        keep = ctx.enter_context(tc.tile_pool(name="keep", bufs=1))
        psum = ctx.enter_context(tc.psum_pool(name="psum", bufs=1))

        k1_t = keep.tile([P, H // 16], U16, name="k1_t")
        offs_t = keep.tile([P, S // 16], U16, name="offs_t")
        n1_t = keep.tile([P, S // 16], U16, name="n1_t")
        n2_t = keep.tile([P, S // 16], U16, name="n2_t")
        n3_t = keep.tile([P, S // 16], U16, name="n3_t")
        n4_t = keep.tile([P, U // 16], U16, name="n4_t")
        d_table = keep.tile([P, TABLE], U32, name="d_table", align_bytes=64)
        x_table = keep.tile([P, TABLE], U32, name="x_table", tag="x_table", align_bytes=64)
        d_stable = keep.tile([P, TABLE], U8, name="d_stable", align_bytes=64)
        nc.sync.dma_start(k1_t[:], k1)
        nc.sync.dma_start(
            d_stable[:].bitcast(I32), d_scales[0].bitcast(I32).unsqueeze(1).to_broadcast([16, 8, TABLE // 4])
        )
        x_stable = keep.tile([P, TABLE], U8, name="x_stable", align_bytes=64)
        nc.sync.dma_start(offs_t[:], offs)
        nc.sync.dma_start(
            x_stable[:].bitcast(I32), x_scales[0].bitcast(I32).unsqueeze(1).to_broadcast([16, 8, TABLE // 4])
        )
        spread = keep.tile([P, H + S + N], U8, name="spread", align_bytes=64)
        nc.sync.dma_start(spread[0:P:8, H + S :].bitcast(I32), w1_scales[0].bitcast(I32))
        sl_t = keep.tile([P, PACK], F32, name="sl_t")
        th_t = keep.tile([P, PACK], F32, name="th_t")
        nc.gpsimd.dma_start(sl_t[:], sl.rearrange("(p t) o -> p (t o)", t=PACK))
        nc.gpsimd.dma_start(th_t[:], th.rearrange("(p t) o -> p (t o)", t=PACK))
        nc.sync.dma_start(d_table[:].bitcast(I32), d_words[0].rearrange("p n t -> p (n t)").bitcast(I32))
        nc.sync.dma_start(n1_t[:], n1)
        nc.sync.dma_start(x_table[:].bitcast(I32), x_words[0].rearrange("p n t -> p (n t)").bitcast(I32))
        nc.sync.dma_start(n2_t[:], n2)
        nc.sync.dma_start(n3_t[:], n3)
        nc.sync.dma_start(n4_t[:], n4)

        planes = keep.tile([P, H + S + N], U8, name="planes", align_bytes=64)
        x_plane = planes[:, H : H + S]

        gn_t = keep.tile([P, PACK], F32, name="gn_t")
        w_codes = keep.tile([P, 2 * N], U8, name="w_codes", align_bytes=64)
        nc.gpsimd.dma_start(gn_t[:], gn.rearrange("(p t) o -> p (t o)", t=PACK))
        nc.gpsimd.dma_start(w_codes[:].bitcast(I32), w1_words[0].bitcast(I32))

        d_sgot = keep.tile([P, H], U8, name="d_sgot", align_bytes=64)
        x_sgot = keep.tile([P, S], U8, name="x_sgot", tag="got", align_bytes=64)
        nc.vector.tensor_copy(d_sgot[:], d_stable[:].indirect(k1_t[:]))
        nc.vector.tensor_copy(
            spread[:, 0:H].rearrange("p (t m) -> p t m", t=PACK), d_sgot[:].rearrange("p (m t) -> p t m", t=PACK)
        )
        nc.vector.tensor_copy(x_sgot[:], x_stable[:].indirect(offs_t[:]))
        nc.vector.tensor_copy(spread[:, H : H + S].bitcast(I32), x_sgot[:].bitcast(I32))
        for q in range(4):
            nc.scalar.dma_start(
                planes[32 * q : 32 * q + 4, :].bitcast(I32), spread[32 * q : 32 * q + 32 : 8, :].bitcast(I32)
            )

        d_got = keep.tile([P, H], U32, name="d_got", tag="got", align_bytes=64)
        d_codes = keep.tile([P, H], U32, name="d_codes", align_bytes=64)
        x_codes = keep.tile([P, S], U32, name="x_codes", tag="got", align_bytes=64)
        nc.vector.tensor_copy(d_got[:], d_table[:].indirect(k1_t[:]))
        nc.vector.tensor_copy(
            d_codes[:].rearrange("p (t c i) -> p c t i", t=PACK, i=4),
            d_got[:].rearrange("p (c i t) -> p c t i", t=PACK, i=4),
        )
        nc.vector.tensor_copy(x_codes[:], x_table[:].indirect(offs_t[:]))

        bias_t = keep.tile([P, PACK], F32, name="bias_t", tag="x_table", align_bytes=64)
        nc.vector.scalar_tensor_tensor(bias_t[:], sl_t[:], -1.0, th_t[:], ALU.mult, ALU.mult)

        h = []
        for t in range(PACK):
            acc = psum.tile([P, S], F32, name="h_acc%d" % t)
            nc.tensor.matmul_mx(
                out=acc[:],
                lhsT=d_codes[:, t * P : (t + 1) * P].bitcast(FP8X4),
                lhsT_scale=planes[:, t * P : (t + 1) * P],
                rhs=x_codes[:].bitcast(FP8X4),
                rhs_scale=x_plane,
                start=True,
                stop=True,
            )
            h_t = keep.tile([P, S], F32, name="h%d" % t)
            nc.vector.tensor_scalar(h_t[:], acc[:], 0.0625, None, ALU.mult)
            h.append(h_t)

        h2_acc = [psum.tile([P, S], F32, name="h2_acc%d" % m) for m in range(TILES)]
        h2 = [keep.tile([P, S], F32, name="h2_%d" % m) for m in range(TILES)]

        def gate(u):
            cols = slice(u * HALF, (u + 1) * HALF)
            sg = keep.tile([P, PACK, HALF], F32, name="sg%d" % u)
            z_rows = keep.tile([P, PACK, HALF], BF16, name="z_rows%d" % u, tag="z%d" % u, align_bytes=64)
            z_woven = keep.tile([P, HALF, PACK], BF16, name="z_woven%d" % u, tag="z%d" % (u + 1), align_bytes=64)
            z_codes = keep.tile([P, HALF], U32, name="z_codes%d" % u, align_bytes=64)
            z_plane = keep.tile([P, HALF], U8, name="z_plane%d" % u, align_bytes=64)
            for t in range(PACK):
                nc.scalar.activation(
                    out=sg[:, t, :],
                    in_=h[t][:].indirect(n1_t[:, u * HALF // 16 : (u + 1) * HALF // 16]),
                    func=ACT.Sigmoid,
                    scale=sl_t[:, t : t + 1],
                    bias=bias_t[:, t : t + 1],
                )
                nc.vector.scalar_tensor_tensor(
                    z_rows[:, t, :], h[t][:, cols], gn_t[:, t : t + 1], sg[:, t, :], ALU.mult, ALU.mult
                )
            nc.vector.tensor_copy(
                z_woven[:].rearrange("p (c i) t -> p c t i", i=4), z_rows[:].rearrange("p t (c i) -> p c t i", i=4)
            )
            nc.vector.quantize_mx(
                out=z_codes[:].bitcast(FP8X4), scales=z_plane[:], in_=z_woven[:].rearrange("p j t -> p (j t)")
            )
            return z_codes, z_plane

        def second_product(u, z_codes, z_plane):
            cols = slice(u * HALF, (u + 1) * HALF)
            for m in range(TILES):
                nc.tensor.matmul_mx(
                    out=h2_acc[m][:, cols],
                    lhsT=w_codes[:, 2 * m * P : 2 * (m + 1) * P].bitcast(FP4X4),
                    lhsT_scale=planes[:, H + S + m * P : H + S + (m + 1) * P],
                    rhs=z_codes[:].bitcast(FP8X4),
                    rhs_scale=z_plane[:],
                    start=True,
                    stop=True,
                )

        second_product(0, *gate(0))
        z_last = gate(1)
        for m in (0, 1):
            nc.scalar.copy(h2[m][:, 0:HALF], h2_acc[m][:, 0:HALF])
        second_product(1, *z_last)
        for m in (0, 1):
            nc.vector.tensor_copy(h2[m][:, HALF:], h2_acc[m][:, HALF:])
        for m in (2, 3):
            nc.vector.tensor_copy(h2[m][:], h2_acc[m][:])

        pg = [keep.tile([P, U], F32, name="pg%d" % m) for m in range(TILES)]

        def scatter(m, places, factor, lo, hi):
            nc.scalar.activation(
                out=pg[m][:].indirect(places[:, lo // 16 : hi // 16]), in_=h2[m][:, lo:hi], func=ACT.Copy, scale=factor
            )

        def finish(m, bounds):
            got = keep.tile([P, U], F32, name="got%d" % m)
            res = keep.tile([P, U], F32, name="res%d" % m)
            for lo, hi in bounds:
                nc.scalar.activation(
                    out=got[:, lo:hi], in_=pg[m][:].indirect(n4_t[:, lo // 16 : hi // 16]), func=ACT.Copy
                )
                nc.vector.tensor_tensor(res[:, lo:hi], pg[m][:, lo:hi], got[:, lo:hi], ALU.subtract)
                nc.sync.dma_start(out[m * P : (m + 1) * P, lo:hi], res[:, lo:hi])

        halves = [(0, 256), (256, 512)]
        for lo in (0, HALF):
            for places, factor in ((n2_t, 1.0), (n3_t, 0.5)):
                for m in (0, 1):
                    scatter(m, places, factor, lo, lo + HALF)
        finish(0, halves)
        scatter(2, n2_t, 1.0, 0, S)
        finish(1, halves)
        scatter(3, n2_t, 1.0, 0, S)
        scatter(2, n3_t, 0.5, 0, S)
        scatter(3, n3_t, 0.5, 0, S)
        finish(2, halves)
        finish(3, [(0, 256), (256, 384), (384, 512)])
